import numpy as np, ml_dtypes
CORES = [25,29,65,69,153,157,193,197]
N = 8
TK = 512
def setup_inputs(rng):
    return {"x": rng.standard_normal((N, 128, TK), dtype=np.float32).astype(ml_dtypes.bfloat16), "w1": (rng.standard_normal((N, 128, 128), dtype=np.float32) / 8).astype(ml_dtypes.bfloat16), "w2": (rng.standard_normal((N, 128, 128), dtype=np.float32) / 8).astype(ml_dtypes.bfloat16)}
def setup_inputs_big(rng):
    d = setup_inputs(rng)
    for k in ("x", "w1", "w2"): d[k] = (d[k].astype(np.float32) * 1024.0).astype(d[k].dtype)
    return d
def setup_inputs_small(rng):
    d = setup_inputs(rng)
    for k in ("x", "w1", "w2"): d[k] = (d[k].astype(np.float32) * (1 / 1024.0)).astype(d[k].dtype)
    return d
def setup_inputs_apart(rng):
    d = setup_inputs(rng)
    f = (10.0 ** rng.permutation(np.linspace(-1.5, 1.5, N))).astype(np.float32).reshape(N, 1, 1)
    for k in ("x", "w1", "w2"): d[k] = (d[k].astype(np.float32) * f).astype(d[k].dtype)
    return d
def reference(x, w1, w2):
    X, W1, W2 = x.astype(np.float64), w1.astype(np.float64), w2.astype(np.float64)
    y = np.zeros((N, 128, TK))
    for r in range(N):
        for j in range(N):
            y[r] += W2[j].T @ np.maximum(W1[j].T @ X[r], 0.0)
    return {"y": y.astype(ml_dtypes.bfloat16 if x.dtype != np.float64 else np.float64)}

@@ -1,0 +1,171 @@
+from concourse.bass import DstId, RemoteDMATransfer
+from concourse.mybir import AluOpType
+
+N = 8
+TK = 512
+D = 128
+WC = 2 * D
+HALF = TK // 2
+HBANKS = 4
+
+SCRATCH = {
+    "wd": ("dram", [D, WC], "bfloat16"),
+    "wall": ("sbuf", [D, N * WC], "bfloat16"),
+    "xs": ("sbuf", [D, TK], "bfloat16"),
+    "zero": ("sbuf", [D, TK], "bfloat16"),
+    "hs": ("sbuf", [D, N * TK], "bfloat16"),
+    "ys": ("sbuf", [D, TK], "bfloat16"),
+    "yp0": ("psum", [D, TK], "float32"),
+    "yp1": ("psum", [D, TK], "float32"),
+}
+for _b in range(HBANKS):
+    SCRATCH["hp%d" % _b] = ("psum", [D, TK], "float32")
+
+SEMAPHORES = (["wdl", "ld", "sent", "zs", "st", "yd0", "yd1", "yc0", "yc1"]
+              + ["arr%d" % j for j in range(N)]
+              + ["m%d" % k for k in range(N)]
+              + ["r%d" % k for k in range(N)])
+
+
+def _chip(topo, c):
+    return (topo.host(c), topo.chip(c))
+
+
+def _count(mask):
+    return bin(mask).count("1")
+
+
+def _split(topo, core, dests):
+    out, taken = [], 0
+    for away in (True, False):
+        ds = [d for d in dests if (_chip(topo, d) != _chip(topo, core)) == away]
+        if ds:
+            m = ~taken
+            for d in ds:
+                m &= topo.mask(core, d)
+            out.append((m, ds))
+            taken |= m
+    return out
+
+
+def _plan(T, topo):
+    ranks = list(T.cores)
+    world = range((max(topo.host(c) for c in ranks) + 1) * topo.CORES_PER_HOST)
+    used = set(ranks)
+    direct, feeds, relay, due = {}, {}, {}, {}
+    for j, s in enumerate(ranks):
+        others = [d for d in ranks if d != s]
+        direct[j] = sorted((d for d in others if topo.may_write(s, d)), key=lambda d: topo.die(d) != topo.die(s))
+        far = sorted((d for d in others if not topo.may_write(s, d)),
+                     key=lambda d: (topo.host(d) != topo.host(s), topo.die(d) != topo.die(s)))
+        feeds[j] = []
+        for d in far:
+            able = [c for c in world if c not in used and topo.die(c) == topo.die(s) and topo.may_write(c, d)]
+            near = [c for c in able if _chip(topo, c) == _chip(topo, s)]
+            there = [c for c in able if topo.same_plane(s, c) and topo.mates(c, d)]
+            h = (near + there)[0]
+            used.add(h)
+            feeds[j].append(h)
+            relay[h] = (j, d)
+        for mask, ds in _split(topo, s, direct[j]):
+            for pos, d in enumerate(ds):
+                due[(d, j)] = (_count(mask), (1, pos, _chip(topo, d) != _chip(topo, s)))
+        for mask, hs in _split(topo, s, feeds[j]):
+            for pos, h in enumerate(hs):
+                due[(h, j)] = (_count(mask), None)
+                d = relay[h][1]
+                due[(d, j)] = (_count(topo.mask(h, d)), (2, pos, _chip(topo, h) != _chip(topo, s)))
+    return direct, feeds, relay, due
+
+
+def _send(g, T, topo, core, j, dests, dst_ap):
+    transfers, n = [], 0
+    for mask, ds in _split(topo, core, dests):
+        ids = []
+        for d in ds:
+            rid, pid = topo.addr(d, core)
+            ids.append(DstId(rid=rid, pnc=pid))
+        transfers.append(RemoteDMATransfer(dst_ids=ids, dma_engine_mask=mask, remote_sem=T.sem["arr%d" % j],
+                                           srcs=[T.wd[:, :]], dsts=[dst_ap for _ in ds], alu_op=0))
+        n += _count(mask)
+    g.remote_dma_fused(transfers, local_sem=T.sem.sent)
+    return n
+
+
+def rank_program(g, core, T, topo):
+    direct, feeds, relay, due = _plan(T, topo)
+    rank = T.rank_of(core)
+
+    if rank is None:
+        if core not in relay:
+            return
+        j, d = relay[core]
+        g.wait_ge(T.sem["arr%d" % j], due[(core, j)][0])
+        n = _send(g, T, topo, core, j, [d], T.wall[:, j * WC:(j + 1) * WC])
+        g.wait_ge(T.sem.sent, n)
+        return
+
+    own = T.wall[:, rank * WC:(rank + 1) * WC]
+
+    g.sync.dma_start(T.wd[:, 0:D], T.w1[:, :]).then_inc(T.sem.wdl, 16)
+    g.scalar.dma_start(T.wd[:, D:WC], T.w2[:, :]).then_inc(T.sem.wdl, 16)
+    g.sync.dma_start(T.wall[:, rank * WC:rank * WC + D], T.w1[:, :]).then_inc(T.sem.ld, 16)
+    g.scalar.dma_start(T.xs[:, :], T.x[:, :]).then_inc(T.sem.ld, 16)
+    g.sync.dma_start(T.wall[:, rank * WC + D:(rank + 1) * WC], T.w2[:, :]).then_inc(T.sem.ld, 16)
+
+    g.wait_ge(T.sem.wdl, 32)
+    n = _send(g, T, topo, core, rank, feeds[rank], T.wd[:, :])
+    n += _send(g, T, topo, core, rank, direct[rank], own)
+
+    early = sorted((j for j in range(N) if j != rank and due[(core, j)][1][0] == 1), key=lambda j: due[(core, j)][1])
+    late = sorted((j for j in range(N) if j != rank and due[(core, j)][1][0] == 2), key=lambda j: due[(core, j)][1])
+    order = [rank] + early + late
+    yp = [T.yp0, T.yp1]
+    yd = [T.sem.yd0, T.sem.yd1]
+    yc = [T.sem.yc0, T.sem.yc1]
+
+    def mm1(k):
+        j = order[k]
+        if j == rank:
+            g.tensor.wait_ge(T.sem.ld, 48)
+        else:
+            g.tensor.wait_ge(T.sem["arr%d" % j], due[(core, j)][0])
+        g.tensor.matmul(T["hp%d" % (k % HBANKS)][:, :], T.wall[:, j * WC:j * WC + D], T.xs[:, :],
+                        True, True).then_inc(T.sem["m%d" % k], 1)
+
+    def mm2(k):
+        j = order[k]
+        g.tensor.wait_ge(T.sem["r%d" % k], 1)
+        for c in range(2):
+            i = g.tensor.matmul(yp[c][:, 0:HALF], T.wall[:, j * WC + D:(j + 1) * WC],
+                                T.hs[:, k * TK + c * HALF:k * TK + (c + 1) * HALF], k == 0, k == N - 1)
+            if k == N - 1:
+                i.then_inc(yd[c], 1)
+
+    first = 0
+    for size, ahead in ((1, 0), (len(early), 1), (len(late), 2)):
+        ks = list(range(first, first + size))
+        for k in ks[:ahead]:
+            mm1(k)
+        for i, k in enumerate(ks):
+            if i + ahead < size:
+                mm1(ks[i + ahead])
+            mm2(k)
+        first += size
+
+    g.vector.memset(T.zero[:, :], 0.0).then_inc(T.sem.zs, 1)
+    g.vector.wait_ge(T.sem.zs, 1)
+    for k in range(N):
+        g.vector.wait_ge(T.sem["m%d" % k], 1)
+        g.vector.tensor_tensor(T.hs[:, k * TK:(k + 1) * TK], T["hp%d" % (k % HBANKS)][:, :], T.zero[:, :],
+                               AluOpType.max).then_inc(T.sem["r%d" % k], 1)
+    for c in range(2):
+        g.vector.wait_ge(yd[c], 1)
+        g.vector.tensor_copy(T.ys[:, c * HALF:(c + 1) * HALF], yp[c][:, 0:HALF]).then_inc(yc[c], 1)
+
+    for c, q in enumerate((g.sync, g.scalar)):
+        q.wait_ge(yc[c], 1)
+        q.dma_start(T.y[:, c * HALF:(c + 1) * HALF], T.ys[:, c * HALF:(c + 1) * HALF]).then_inc(T.sem.st, 16)
+
+    g.wait_ge(T.sem.sent, n)
+    g.wait_ge(T.sem.st, 32)

@@ -9,7 +9,8 @@ HALF = TK // 2
 HBANKS = 4
 
 SCRATCH = {
-    "wd": ("dram", [D, WC], "bfloat16"),
+    "wd1": ("dram", [D, D], "bfloat16"),
+    "wd2": ("dram", [D, D], "bfloat16"),
     "wall": ("sbuf", [D, N * WC], "bfloat16"),
     "xs": ("sbuf", [D, TK], "bfloat16"),
     "zero": ("sbuf", [D, TK], "bfloat16"),
@@ -21,8 +22,9 @@ SCRATCH = {
 for _b in range(HBANKS):
     SCRATCH["hp%d" % _b] = ("psum", [D, TK], "float32")
 
-SEMAPHORES = (["wdl", "ld", "sent", "zs", "st", "yd0", "yd1", "yc0", "yc1"]
+SEMAPHORES = (["wl1", "wl2", "ld", "sent", "zs", "st", "yd0", "yd1", "yc0", "yc1"]
               + ["arr%d" % j for j in range(N)]
+              + ["brr%d" % j for j in range(N)]
               + ["m%d" % k for k in range(N)]
               + ["r%d" % k for k in range(N)])
 
@@ -67,26 +69,28 @@ def _plan(T, topo):
             used.add(h)
             feeds[j].append(h)
             relay[h] = (j, d)
-        for mask, ds in _split(topo, s, direct[j]):
-            for pos, d in enumerate(ds):
-                due[(d, j)] = (_count(mask), (1, pos, _chip(topo, d) != _chip(topo, s)))
-        for mask, hs in _split(topo, s, feeds[j]):
-            for pos, h in enumerate(hs):
-                due[(h, j)] = (_count(mask), None)
-                d = relay[h][1]
-                due[(d, j)] = (_count(topo.mask(h, d)), (2, pos, _chip(topo, h) != _chip(topo, s)))
+        for mask, cs in _split(topo, s, feeds[j] + direct[j]):
+            for pos, c in enumerate(cs):
+                away = _chip(topo, c) != _chip(topo, s)
+                if c in relay:
+                    due[(c, j)] = (_count(mask), None)
+                    d = relay[c][1]
+                    due[(d, j)] = (_count(topo.mask(c, d)), (2, pos, away))
+                else:
+                    due[(c, j)] = (_count(mask), (1, pos, away))
     return direct, feeds, relay, due
 
 
-def _send(g, T, topo, core, j, dests, dst_ap):
+def _send(g, T, topo, core, sem, src, dests):
+    where = dict(dests)
     transfers, n = [], 0
-    for mask, ds in _split(topo, core, dests):
+    for mask, ds in _split(topo, core, [d for d, _ in dests]):
         ids = []
         for d in ds:
             rid, pid = topo.addr(d, core)
             ids.append(DstId(rid=rid, pnc=pid))
-        transfers.append(RemoteDMATransfer(dst_ids=ids, dma_engine_mask=mask, remote_sem=T.sem["arr%d" % j],
-                                           srcs=[T.wd[:, :]], dsts=[dst_ap for _ in ds], alu_op=0))
+        transfers.append(RemoteDMATransfer(dst_ids=ids, dma_engine_mask=mask, remote_sem=sem,
+                                           srcs=[src], dsts=[where[d] for d in ds], alu_op=0))
         n += _count(mask)
     g.remote_dma_fused(transfers, local_sem=T.sem.sent)
     return n
@@ -100,22 +104,25 @@ def rank_program(g, core, T, topo):
         if core not in relay:
             return
         j, d = relay[core]
-        g.wait_ge(T.sem["arr%d" % j], due[(core, j)][0])
-        n = _send(g, T, topo, core, j, [d], T.wall[:, j * WC:(j + 1) * WC])
+        n = 0
+        for name, src, lo in (("arr%d", T.wd1, 0), ("brr%d", T.wd2, D)):
+            g.wait_ge(T.sem[name % j], due[(core, j)][0])
+            n += _send(g, T, topo, core, T.sem[name % j], src[:, :], [(d, T.wall[:, j * WC + lo:j * WC + lo + D])])
         g.wait_ge(T.sem.sent, n)
         return
 
-    own = T.wall[:, rank * WC:(rank + 1) * WC]
-
-    g.sync.dma_start(T.wd[:, 0:D], T.w1[:, :]).then_inc(T.sem.wdl, 16)
-    g.scalar.dma_start(T.wd[:, D:WC], T.w2[:, :]).then_inc(T.sem.wdl, 16)
+    g.sync.dma_start(T.wd1[:, :], T.w1[:, :]).then_inc(T.sem.wl1, 16)
+    g.scalar.dma_start(T.wd2[:, :], T.w2[:, :]).then_inc(T.sem.wl2, 16)
     g.sync.dma_start(T.wall[:, rank * WC:rank * WC + D], T.w1[:, :]).then_inc(T.sem.ld, 16)
     g.scalar.dma_start(T.xs[:, :], T.x[:, :]).then_inc(T.sem.ld, 16)
     g.sync.dma_start(T.wall[:, rank * WC + D:(rank + 1) * WC], T.w2[:, :]).then_inc(T.sem.ld, 16)
 
-    g.wait_ge(T.sem.wdl, 32)
-    n = _send(g, T, topo, core, rank, feeds[rank], T.wd[:, :])
-    n += _send(g, T, topo, core, rank, direct[rank], own)
+    n = 0
+    for ready, name, src, lo in ((T.sem.wl1, "arr%d", T.wd1, 0), (T.sem.wl2, "brr%d", T.wd2, D)):
+        g.wait_ge(ready, 16)
+        n += _send(g, T, topo, core, T.sem[name % rank], src[:, :],
+                   [(h, src[:, :]) for h in feeds[rank]]
+                   + [(d, T.wall[:, rank * WC + lo:rank * WC + lo + D]) for d in direct[rank]])
 
     early = sorted((j for j in range(N) if j != rank and due[(core, j)][1][0] == 1), key=lambda j: due[(core, j)][1])
     late = sorted((j for j in range(N) if j != rank and due[(core, j)][1][0] == 2), key=lambda j: due[(core, j)][1])
@@ -135,6 +142,8 @@ def rank_program(g, core, T, topo):
 
     def mm2(k):
         j = order[k]
+        if j != rank:
+            g.tensor.wait_ge(T.sem["brr%d" % j], due[(core, j)][0])
         g.tensor.wait_ge(T.sem["r%d" % k], 1)
         for c in range(2):
             i = g.tensor.matmul(yp[c][:, 0:HALF], T.wall[:, j * WC + D:(j + 1) * WC],
@@ -143,13 +152,11 @@ def rank_program(g, core, T, topo):
                 i.then_inc(yd[c], 1)
 
     first = 0
-    for size, ahead in ((1, 0), (len(early), 1), (len(late), 2)):
+    for size in (1, len(early), len(late)):
         ks = list(range(first, first + size))
-        for k in ks[:ahead]:
+        for k in ks:
             mm1(k)
-        for i, k in enumerate(ks):
-            if i + ahead < size:
-                mm1(ks[i + ahead])
+        for k in ks:
             mm2(k)
         first += size
 

from concourse.bass import DstId, RemoteDMATransfer
from concourse.mybir import AluOpType

N = 8
TK = 512
D = 128
WC = 2 * D
HALF = TK // 2
HBANKS = 4

SCRATCH = {
    "wd1": ("dram", [D, D], "bfloat16"),
    "wd2": ("dram", [D, D], "bfloat16"),
    "wall": ("sbuf", [D, N * WC], "bfloat16"),
    "xs": ("sbuf", [D, TK], "bfloat16"),
    "zero": ("sbuf", [D, TK], "bfloat16"),
    "hs": ("sbuf", [D, N * TK], "bfloat16"),
    "ys": ("sbuf", [D, TK], "bfloat16"),
    "yp0": ("psum", [D, TK], "float32"),
    "yp1": ("psum", [D, TK], "float32"),
}
for _b in range(HBANKS):
    SCRATCH["hp%d" % _b] = ("psum", [D, TK], "float32")

SEMAPHORES = (["wl1", "wl2", "ld", "sent", "zs", "st", "yd0", "yd1", "yc0", "yc1"]
              + ["arr%d" % j for j in range(N)]
              + ["brr%d" % j for j in range(N)]
              + ["m%d" % k for k in range(N)]
              + ["r%d" % k for k in range(N)])


def _chip(topo, c):
    return (topo.host(c), topo.chip(c))


def _count(mask):
    return bin(mask).count("1")


def _split(topo, core, dests):
    out, taken = [], 0
    for away in (True, False):
        ds = [d for d in dests if (_chip(topo, d) != _chip(topo, core)) == away]
        if ds:
            m = ~taken
            for d in ds:
                m &= topo.mask(core, d)
            out.append((m, ds))
            taken |= m
    return out


def _plan(T, topo):
    ranks = list(T.cores)
    world = range((max(topo.host(c) for c in ranks) + 1) * topo.CORES_PER_HOST)
    used = set(ranks)
    direct, feeds, relay, due = {}, {}, {}, {}
    for j, s in enumerate(ranks):
        others = [d for d in ranks if d != s]
        direct[j] = sorted((d for d in others if topo.may_write(s, d)), key=lambda d: topo.die(d) != topo.die(s))
        far = sorted((d for d in others if not topo.may_write(s, d)),
                     key=lambda d: (topo.host(d) != topo.host(s), topo.die(d) != topo.die(s)))
        feeds[j] = []
        for d in far:
            able = [c for c in world if c not in used and topo.die(c) == topo.die(s) and topo.may_write(c, d)]
            near = [c for c in able if _chip(topo, c) == _chip(topo, s)]
            there = [c for c in able if topo.same_plane(s, c) and topo.mates(c, d)]
            h = (near + there)[0]
            used.add(h)
            feeds[j].append(h)
            relay[h] = (j, d)
        for mask, cs in _split(topo, s, feeds[j] + direct[j]):
            for pos, c in enumerate(cs):
                away = _chip(topo, c) != _chip(topo, s)
                if c in relay:
                    due[(c, j)] = (_count(mask), None)
                    d = relay[c][1]
                    due[(d, j)] = (_count(topo.mask(c, d)), (2, pos, away))
                else:
                    due[(c, j)] = (_count(mask), (1, pos, away))
    return direct, feeds, relay, due


def _send(g, T, topo, core, sem, src, dests):
    where = dict(dests)
    transfers, n = [], 0
    for mask, ds in _split(topo, core, [d for d, _ in dests]):
        ids = []
        for d in ds:
            rid, pid = topo.addr(d, core)
            ids.append(DstId(rid=rid, pnc=pid))
        transfers.append(RemoteDMATransfer(dst_ids=ids, dma_engine_mask=mask, remote_sem=sem,
                                           srcs=[src], dsts=[where[d] for d in ds], alu_op=0))
        n += _count(mask)
    g.remote_dma_fused(transfers, local_sem=T.sem.sent)
    return n


def rank_program(g, core, T, topo):
    direct, feeds, relay, due = _plan(T, topo)
    rank = T.rank_of(core)

    if rank is None:
        if core not in relay:
            return
        j, d = relay[core]
        n = 0
        for name, src, lo in (("arr%d", T.wd1, 0), ("brr%d", T.wd2, D)):
            g.wait_ge(T.sem[name % j], due[(core, j)][0])
            n += _send(g, T, topo, core, T.sem[name % j], src[:, :], [(d, T.wall[:, j * WC + lo:j * WC + lo + D])])
        g.wait_ge(T.sem.sent, n)
        return

    g.sync.dma_start(T.wd1[:, :], T.w1[:, :]).then_inc(T.sem.wl1, 16)
    g.scalar.dma_start(T.wd2[:, :], T.w2[:, :]).then_inc(T.sem.wl2, 16)
    g.sync.dma_start(T.wall[:, rank * WC:rank * WC + D], T.w1[:, :]).then_inc(T.sem.ld, 16)
    g.scalar.dma_start(T.xs[:, :], T.x[:, :]).then_inc(T.sem.ld, 16)
    g.sync.dma_start(T.wall[:, rank * WC + D:(rank + 1) * WC], T.w2[:, :]).then_inc(T.sem.ld, 16)

    n = 0
    for ready, name, src, lo in ((T.sem.wl1, "arr%d", T.wd1, 0), (T.sem.wl2, "brr%d", T.wd2, D)):
        g.wait_ge(ready, 16)
        n += _send(g, T, topo, core, T.sem[name % rank], src[:, :],
                   [(h, src[:, :]) for h in feeds[rank]]
                   + [(d, T.wall[:, rank * WC + lo:rank * WC + lo + D]) for d in direct[rank]])

    early = sorted((j for j in range(N) if j != rank and due[(core, j)][1][0] == 1), key=lambda j: due[(core, j)][1])
    late = sorted((j for j in range(N) if j != rank and due[(core, j)][1][0] == 2), key=lambda j: due[(core, j)][1])
    order = [rank] + early + late
    yp = [T.yp0, T.yp1]
    yd = [T.sem.yd0, T.sem.yd1]
    yc = [T.sem.yc0, T.sem.yc1]

    def mm1(k):
        j = order[k]
        if j == rank:
            g.tensor.wait_ge(T.sem.ld, 48)
        else:
            g.tensor.wait_ge(T.sem["arr%d" % j], due[(core, j)][0])
        g.tensor.matmul(T["hp%d" % (k % HBANKS)][:, :], T.wall[:, j * WC:j * WC + D], T.xs[:, :],
                        True, True).then_inc(T.sem["m%d" % k], 1)

    def mm2(k):
        j = order[k]
        if j != rank:
            g.tensor.wait_ge(T.sem["brr%d" % j], due[(core, j)][0])
        g.tensor.wait_ge(T.sem["r%d" % k], 1)
        for c in range(2):
            i = g.tensor.matmul(yp[c][:, 0:HALF], T.wall[:, j * WC + D:(j + 1) * WC],
                                T.hs[:, k * TK + c * HALF:k * TK + (c + 1) * HALF], k == 0, k == N - 1)
            if k == N - 1:
                i.then_inc(yd[c], 1)

    first = 0
    for size in (1, len(early), len(late)):
        ks = list(range(first, first + size))
        for k in ks:
            mm1(k)
        for k in ks:
            mm2(k)
        first += size

    g.vector.memset(T.zero[:, :], 0.0).then_inc(T.sem.zs, 1)
    g.vector.wait_ge(T.sem.zs, 1)
    for k in range(N):
        g.vector.wait_ge(T.sem["m%d" % k], 1)
        g.vector.tensor_tensor(T.hs[:, k * TK:(k + 1) * TK], T["hp%d" % (k % HBANKS)][:, :], T.zero[:, :],
                               AluOpType.max).then_inc(T.sem["r%d" % k], 1)
    for c in range(2):
        g.vector.wait_ge(yd[c], 1)
        g.vector.tensor_copy(T.ys[:, c * HALF:(c + 1) * HALF], yp[c][:, 0:HALF]).then_inc(yc[c], 1)

    for c, q in enumerate((g.sync, g.scalar)):
        q.wait_ge(yc[c], 1)
        q.dma_start(T.y[:, c * HALF:(c + 1) * HALF], T.ys[:, c * HALF:(c + 1) * HALF]).then_inc(T.sem.st, 16)

    g.wait_ge(T.sem.sent, n)
    g.wait_ge(T.sem.st, 32)
